import numpy as np
import ml_dtypes


def mxq(x, axis, fmt="e4m3"):
    dtype, down = {"e4m3": (ml_dtypes.float8_e4m3fn, 7), "e5m2": (ml_dtypes.float8_e5m2, 14)}[fmt]
    v = np.moveaxis(np.asarray(x, np.float32).astype(ml_dtypes.bfloat16).astype(np.float64), axis, -1)
    blocks = v.reshape(v.shape[:-1] + (-1, 32))
    amax = np.abs(blocks).max(-1, keepdims=True)
    byte = np.maximum(np.where(amax > 0, np.frexp(amax)[1] - 1 + 127, 0) - down, 1)
    scale = np.exp2(byte - 127.0)
    codes = (blocks / scale).astype(np.float32).astype(dtype).astype(np.float64)
    return np.moveaxis((codes * scale).reshape(v.shape), -1, axis)


WIDE = False


def mx_kscale(k, group=512):
    if not WIDE:
        return np.ones(k)
    levels = np.array([18, -18])
    if group != 512:
        return np.exp2(np.random.permutation(np.resize(levels, k // group))).repeat(group)
    if k % 512:
        return np.exp2(np.random.permutation(np.resize(levels, k // 32))).repeat(32)
    a = np.empty((k // 512, 16))
    for p in range(k // 512):
        a[p, :8] = np.random.permutation(np.resize(levels, 8))
        for g in range(8):
            far = levels[np.abs(levels - a[p, g]) >= 10]
            a[p, g + 8] = far[np.random.randint(len(far))]
    return np.exp2(a.ravel()).repeat(32)


def f64(x):
    return np.asarray(x).astype(np.float64)


def sigmoid(v):
    return 1.0 / (1.0 + np.exp(-v))


G, D, M, O, N = 4, 128, 128, 128, 512


def sgn(shape):
    return np.random.uniform(0.5, 2.0, shape) * np.where(np.random.standard_normal(shape) < 0, -1.0, 1.0)


def setup_inputs():
    n = np.random.standard_normal
    s_d = mx_kscale(D, 0)
    s_m = mx_kscale(M, 0)
    return {
        "x": (n((G, D, N)) * s_d[:, None]).astype(np.float32),
        "w1": (n((G, D, M)) / np.sqrt(D) / s_d[:, None]).astype(np.float32),
        "w2": (n((G, D, M)) / np.sqrt(D) / s_d[:, None]).astype(np.float32),
        "w3": (n((G, D, M)) / np.sqrt(D) / s_d[:, None]).astype(np.float32),
        "hs": (sgn((G, M, 1)) * s_m[:, None]).astype(np.float32),
        "wo2": (n((G, M, O)) / np.sqrt(M) / s_m[:, None]).astype(np.float32),
        "res": (0.5 * n((G, O, N))).astype(np.float32),
    }


def reference(x, w1, w2, w3, hs, wo2, res):
    w1q = mxq(f64(w1), 1, "e4m3")
    xq = mxq(f64(x), 1, "e4m3")
    z1 = w1q.transpose(0, 2, 1) @ xq
    w2q = mxq(f64(w2), 1, "e4m3")
    z2 = w2q.transpose(0, 2, 1) @ xq
    w3q = mxq(f64(w3), 1, "e4m3")
    z3 = w3q.transpose(0, 2, 1) @ xq
    sg = sigmoid(z1 * z2 + z3)
    h = sg * np.tanh(z3)
    hh = h * f64(hs)
    wo2q = mxq(f64(wo2), 1, "e4m3")
    hhq = mxq(hh, 1, "e4m3")
    y0 = wo2q.transpose(0, 2, 1) @ hhq
    y = y0 + f64(res)
    return y

@@ -1,0 +1,259 @@
+from contextlib import ExitStack
+
+import concourse.mybir as mybir
+
+G, D, M, O, N = 4, 128, 128, 128, 512
+FLOPS = 2 * G * N * (3 * D * M + M * O)
+
+F32 = mybir.dt.float32
+BF16 = mybir.dt.bfloat16
+U32 = mybir.dt.uint32
+U8 = mybir.dt.uint8
+FP8X4 = mybir.dt.float8_e4m3fn_x4
+ACT = mybir.ActivationFunctionType
+ALU = mybir.AluOpType
+
+P = 128
+PACK = 4
+ROWS = 32
+NMM = 128
+HALF = 256
+WIDTHS = (128, 256, 128)
+X1_VECTOR = 160
+H1_VECTOR = 160
+
+
+def tile_rows_fbilinsig_kernel(tc, x, w1, w2, w3, hs, wo2, res, out):
+    nc = tc.nc
+    starts = [sum(WIDTHS[:c]) for c in range(len(WIDTHS))]
+    steps = [(c, g) for c in range(len(WIDTHS)) for g in range(G)]
+
+    with ExitStack() as ctx:
+        sb = ctx.enter_context(tc.tile_pool(name="sb", bufs=1))
+        ps = ctx.enter_context(tc.psum_pool(name="ps", bufs=1))
+        ctx.enter_context(tc.manual_schedule())
+
+        def load_rows(name, src):
+            width = src.shape[2]
+            raw = sb.tile([P, PACK, width], F32, name=name + "_raw")
+            nc.sync.dma_start(out=raw[:], in_=src)
+            return raw
+
+        def k_rows(t):
+            return t.rearrange("g (p j) c -> (g p) j c", j=PACK)
+
+        def packed_tile(name, width):
+            return sb.tile([P, width, PACK], BF16, name=name + "_packed", align_bytes=64)
+
+        def interleave(copy, packed, raw, c0, c1):
+            copy(out=packed[:, c0:c1, :].rearrange("p (c i) j -> p c j i", i=4),
+                 in_=raw[:, :, c0:c1].rearrange("p j (c i) -> p c j i", i=4))
+
+        def quantize(name, packed):
+            width = packed.shape[1]
+            codes = sb.tile([P, width], U32, name=name + "_codes", align_bytes=64)
+            scales = sb.tile([P, width], U8, name=name + "_scales", align_bytes=64)
+            nc.vector.quantize_mx(out=codes[:].bitcast(FP8X4), scales=scales[:],
+                                  in_=packed[:].rearrange("p c j -> p (c j)"))
+            return codes, scales
+
+        def product(dst, col0, weights, moving, g, width):
+            rows = slice(ROWS * g, ROWS * (g + 1))
+            for n0 in range(0, width, NMM):
+                nc.tensor.matmul_mx(
+                    out=dst[:, col0 + n0:col0 + n0 + NMM],
+                    lhsT=weights[0][rows, :].bitcast(FP8X4), lhsT_scale=weights[1][rows, :],
+                    rhs=moving[0][rows, n0:n0 + NMM].bitcast(FP8X4), rhs_scale=moving[1][rows, n0:n0 + NMM],
+                    start=True, stop=True)
+
+        bank_a = [ps.tile([P, 512], F32, name="bank_a%d" % g) for g in range(G)]
+        bank_b = [ps.tile([P, 512], F32, name="bank_b%d" % g) for g in range(G)]
+
+        hs_rows = sb.tile([P, G, ROWS], F32, name="hs_rows", align_bytes=64)
+        hs_cols = sb.tile([P, P], F32, name="hs_cols", align_bytes=64)
+        nc.vector.memset(hs_rows[:], 0.0)
+        nc.scalar.dma_start(out=hs_rows[0:P:ROWS, :, :],
+                            in_=hs.rearrange("g (b r) o -> b g (r o)", r=ROWS))
+
+        x_rows = k_rows(x)
+        x_raw = {}
+        w2_raw = load_rows("w2", k_rows(w2))
+        x_raw[0] = load_rows("x0", x_rows[:, :, starts[0]:starts[0] + WIDTHS[0]])
+        w1_raw = load_rows("w1", k_rows(w1))
+        w3_raw = load_rows("w3", k_rows(w3))
+        x_raw[1] = load_rows("x1", x_rows[:, :, starts[1]:starts[1] + WIDTHS[1]])
+        x_raw[2] = load_rows("x2", x_rows[:, :, starts[2]:starts[2] + WIDTHS[2]])
+        wo_raw = load_rows("wo", k_rows(wo2))
+
+        res_t, rows_t = {}, {}
+
+        def load_res(c):
+            res_t[c] = sb.tile([P, G, WIDTHS[c]], F32, name="res%d" % c)
+            nc.sync.dma_start(out=res_t[c][:],
+                              in_=res.rearrange("g o n -> o g n")[:, :, starts[c]:starts[c] + WIDTHS[c]])
+
+        load_res(0)
+
+        def prepare(name, raw):
+            packed = packed_tile(name, raw.shape[2])
+            interleave(nc.vector.tensor_copy, packed, raw, 0, raw.shape[2])
+            return quantize(name, packed)
+
+        nc.vector.transpose(out=hs_cols[:], in_=hs_rows[:].rearrange("p g r -> p (g r)"))
+        xq = {}
+        w2q = prepare("w2", w2_raw)
+        xq[0] = prepare("x0", x_raw[0])
+        z2s, tt, uu, th, sg = {}, {}, {}, {}, {}
+
+        def work(name, s, dtype=F32):
+            return sb.tile([P, WIDTHS[steps[s][0]]], dtype, name="%s%d" % (name, s))
+
+        def mm_z2(s):
+            c, g = steps[s]
+            product(bank_a[g], 0, w2q, xq[c], g, WIDTHS[c])
+
+        def mm_z1(s):
+            c, g = steps[s]
+            product(bank_b[g], 0, w1q, xq[c], g, WIDTHS[c])
+
+        def mm_z3(s):
+            c, g = steps[s]
+            product(bank_a[g], HALF, w3q, xq[c], g, WIDTHS[c])
+
+        def copy_z2(s):
+            c, g = steps[s]
+            z2s[s] = work("z2s", s)
+            nc.scalar.copy(out=z2s[s][:], in_=bank_a[g][:, 0:WIDTHS[c]])
+
+        def tanh_z3(s):
+            c, g = steps[s]
+            th[s] = work("th", s)
+            nc.scalar.activation(out=th[s][:], in_=bank_a[g][:, HALF:HALF + WIDTHS[c]], func=ACT.Tanh)
+
+        def mul_z1(s):
+            c, g = steps[s]
+            tt[s] = work("tt", s)
+            nc.vector.tensor_tensor(out=tt[s][:], in0=bank_b[g][:, 0:WIDTHS[c]], in1=z2s[s][:], op=ALU.mult)
+
+        def add_z3(s):
+            c, g = steps[s]
+            uu[s] = work("uu", s)
+            nc.vector.tensor_tensor(out=uu[s][:], in0=bank_a[g][:, HALF:HALF + WIDTHS[c]], in1=tt[s][:], op=ALU.add)
+
+        def sigmoid(s):
+            sg[s] = work("sg", s)
+            nc.scalar.activation(out=sg[s][:], in_=uu[s][:], func=ACT.Sigmoid)
+
+        def gate(s):
+            c, g = steps[s]
+            hh = work("hh", s, BF16)
+            nc.vector.scalar_tensor_tensor(out=hh[:], in0=sg[s][:], scalar=hs_cols[:, ROWS * g:ROWS * g + 1],
+                                           in1=th[s][:], op0=ALU.mult, op1=ALU.mult)
+            if g == 0:
+                rows_t[c] = sb.tile([P, PACK, WIDTHS[c]], BF16, name="hh_rows%d" % c)
+            nc.sync.dma_start(out=rows_t[c][ROWS * g:ROWS * (g + 1), :, :], in_=hh[:])
+            if g == G - 1 and c + 1 < len(WIDTHS):
+                load_res(c + 1)
+
+        def y_bank(c, g):
+            return bank_a[g] if c % 2 else bank_b[g]
+
+        def mm_y(c, hq):
+            for g in range(G):
+                product(y_bank(c, g), HALF, woq, hq, g, WIDTHS[c])
+
+        y = {}
+
+        def add_res(c, g):
+            if g == 0:
+                y[c] = sb.tile([P, G, WIDTHS[c]], F32, name="y%d" % c)
+            nc.vector.tensor_tensor(out=y[c][:, g, :], in0=y_bank(c, g)[:, HALF:HALF + WIDTHS[c]],
+                                    in1=res_t[c][:, g, :], op=ALU.add)
+
+        def store(c, g0, g1):
+            nc.sync.dma_start(out=out.rearrange("g o n -> o g n")[:, g0:g1, starts[c]:starts[c] + WIDTHS[c]],
+                              in_=y[c][:, g0:g1, :])
+
+        for s in range(G):
+            mm_z2(s)
+        w1q = prepare("w1", w1_raw)
+        for s in range(G):
+            copy_z2(s)
+        for s in range(G):
+            mm_z1(s)
+        w3q = prepare("w3", w3_raw)
+        for s in range(G):
+            mm_z3(s)
+        tanh_z3(0)
+
+        packed = {}
+        last = len(steps) - 1
+        for s in range(last + 3):
+            if s <= last:
+                mul_z1(s)
+            if s + 1 <= last:
+                if s + 1 >= G:
+                    copy_z2(s + 1)
+                tanh_z3(s + 1)
+            if 0 <= s - 2:
+                gate(s - 2)
+            if s <= last:
+                add_z3(s)
+            if 0 <= s - 1 <= last:
+                sigmoid(s - 1)
+            if s == 0:
+                packed["x1"] = packed_tile("x1", WIDTHS[1])
+                interleave(nc.vector.tensor_copy, packed["x1"], x_raw[1], 0, X1_VECTOR)
+                interleave(nc.scalar.copy, packed["x1"], x_raw[1], X1_VECTOR, WIDTHS[1])
+            if s == 1:
+                xq[1] = quantize("x1", packed["x1"])
+                mm_z2(G)
+                mm_z3(G)
+                mm_z1(G)
+            if s == 3:
+                packed["x2"] = packed_tile("x2", WIDTHS[2])
+                interleave(nc.scalar.copy, packed["x2"], x_raw[2], 0, WIDTHS[2])
+            if s == 4:
+                xq[2] = quantize("x2", packed["x2"])
+            if s == 5:
+                packed["wo"] = packed_tile("wo", O)
+                interleave(nc.scalar.copy, packed["wo"], wo_raw, 0, O)
+            if s == 6:
+                woq = quantize("wo", packed["wo"])
+            if s == 8:
+                packed["h0"] = packed_tile("h0", WIDTHS[0])
+                interleave(nc.scalar.copy, packed["h0"], rows_t[0], 0, WIDTHS[0])
+            if s == 10:
+                h0q = quantize("h0", packed["h0"])
+            if s >= 1 and s + G <= last:
+                mm_z2(s + G)
+                mm_z3(s + G)
+                mm_z1(s + G)
+        mm_y(0, h0q)
+
+        packed["h1"] = packed_tile("h1", WIDTHS[1])
+        interleave(nc.vector.tensor_copy, packed["h1"], rows_t[1], 0, H1_VECTOR)
+        interleave(nc.scalar.copy, packed["h1"], rows_t[1], H1_VECTOR, WIDTHS[1])
+        add_res(0, 0)
+        add_res(0, 1)
+        h1q = quantize("h1", packed["h1"])
+        add_res(0, 2)
+        add_res(0, 3)
+        store(0, 0, G)
+        mm_y(1, h1q)
+        packed["h2"] = packed_tile("h2", WIDTHS[2])
+        interleave(nc.scalar.copy, packed["h2"], rows_t[2], 0, WIDTHS[2])
+        add_res(1, 0)
+        add_res(1, 1)
+        store(1, 0, 2)
+        h2q = quantize("h2", packed["h2"])
+        add_res(1, 2)
+        add_res(1, 3)
+        store(1, 2, G)
+        mm_y(2, h2q)
+        add_res(2, 0)
+        add_res(2, 1)
+        store(2, 0, 2)
+        add_res(2, 2)
+        add_res(2, 3)
+        store(2, 2, G)

@@ -17,15 +17,12 @@ P = 128
 PACK = 4
 ROWS = 32
 NMM = 128
-HALF = 256
-WIDTHS = (128, 256, 128)
-X1_VECTOR = 160
-H1_VECTOR = 160
+WIDTHS = (256, 128, 128)
+STARTS = (0, 256, 384)
 
 
 def tile_rows_fbilinsig_kernel(tc, x, w1, w2, w3, hs, wo2, res, out):
     nc = tc.nc
-    starts = [sum(WIDTHS[:c]) for c in range(len(WIDTHS))]
     steps = [(c, g) for c in range(len(WIDTHS)) for g in range(G)]
 
     with ExitStack() as ctx:
@@ -34,20 +31,26 @@ def tile_rows_fbilinsig_kernel(tc, x, w1, w2, w3, hs, wo2, res, out):
         ctx.enter_context(tc.manual_schedule())
 
         def load_rows(name, src):
-            width = src.shape[2]
-            raw = sb.tile([P, PACK, width], F32, name=name + "_raw")
+            raw = sb.tile([P, PACK, src.shape[2]], F32, name=name + "_raw")
             nc.sync.dma_start(out=raw[:], in_=src)
             return raw
 
         def k_rows(t):
             return t.rearrange("g (p j) c -> (g p) j c", j=PACK)
 
-        def packed_tile(name, width):
-            return sb.tile([P, width, PACK], BF16, name=name + "_packed", align_bytes=64)
-
         def interleave(copy, packed, raw, c0, c1):
             copy(out=packed[:, c0:c1, :].rearrange("p (c i) j -> p c j i", i=4),
                  in_=raw[:, :, c0:c1].rearrange("p j (c i) -> p c j i", i=4))
+
+        def pack(name, raw, eighths):
+            width = raw.shape[2]
+            packed = sb.tile([P, width, PACK], BF16, name=name + "_packed", align_bytes=64)
+            cut = width * eighths // 8
+            if cut > 0:
+                interleave(nc.vector.tensor_copy, packed, raw, 0, cut)
+            if cut < width:
+                interleave(nc.scalar.copy, packed, raw, cut, width)
+            return packed
 
         def quantize(name, packed):
             width = packed.shape[1]
@@ -57,88 +60,78 @@ def tile_rows_fbilinsig_kernel(tc, x, w1, w2, w3, hs, wo2, res, out):
                                   in_=packed[:].rearrange("p c j -> p (c j)"))
             return codes, scales
 
-        def product(dst, col0, weights, moving, g, width):
-            rows = slice(ROWS * g, ROWS * (g + 1))
+        def product(dsts, weights, moving, groups):
+            width = moving[0].shape[1]
             for n0 in range(0, width, NMM):
-                nc.tensor.matmul_mx(
-                    out=dst[:, col0 + n0:col0 + n0 + NMM],
-                    lhsT=weights[0][rows, :].bitcast(FP8X4), lhsT_scale=weights[1][rows, :],
-                    rhs=moving[0][rows, n0:n0 + NMM].bitcast(FP8X4), rhs_scale=moving[1][rows, n0:n0 + NMM],
-                    start=True, stop=True)
+                for g in groups:
+                    rows = slice(ROWS * g, ROWS * (g + 1))
+                    nc.tensor.matmul_mx(
+                        out=dsts(g)[:, n0:n0 + NMM],
+                        lhsT=weights[0][rows, :].bitcast(FP8X4), lhsT_scale=weights[1][rows, :],
+                        rhs=moving[0][rows, n0:n0 + NMM].bitcast(FP8X4), rhs_scale=moving[1][rows, n0:n0 + NMM],
+                        start=True, stop=True)
 
-        bank_a = [ps.tile([P, 512], F32, name="bank_a%d" % g) for g in range(G)]
-        bank_b = [ps.tile([P, 512], F32, name="bank_b%d" % g) for g in range(G)]
+        banks = [[ps.tile([P, 512], F32, name="bank%d_%d" % (b, g)) for g in range(G)] for b in range(2)]
+        z_place = {0: ((1, 0), (0, 0), (0, 256)), 1: ((1, 0), (1, 128), (1, 256)), 2: ((0, 0), (0, 128), (0, 256))}
+        y_place = {0: (1, 0), 1: (0, 0), 2: (1, 256)}
 
+        def z_at(c, i, g):
+            b, col = z_place[c][i]
+            return banks[b][g][:, col:col + WIDTHS[c]]
+
+        def y_at(c, g):
+            b, col = y_place[c]
+            return banks[b][g][:, col:col + WIDTHS[c]]
+
+        warm_in = sb.tile([P, 1], F32, name="warm_in")
+        warm_out = sb.tile([P, 1], F32, name="warm_out")
         hs_rows = sb.tile([P, G, ROWS], F32, name="hs_rows", align_bytes=64)
         hs_cols = sb.tile([P, P], F32, name="hs_cols", align_bytes=64)
-        nc.vector.memset(hs_rows[:], 0.0)
-        nc.scalar.dma_start(out=hs_rows[0:P:ROWS, :, :],
-                            in_=hs.rearrange("g (b r) o -> b g (r o)", r=ROWS))
+        nc.gpsimd.memset(hs_rows[:], 0.0)
+        nc.vector.memset(warm_in[:], 0.0)
+        nc.scalar.activation(out=warm_out[:], in_=warm_in[:], func=ACT.Sigmoid)
 
         x_rows = k_rows(x)
-        x_raw = {}
-        w2_raw = load_rows("w2", k_rows(w2))
-        x_raw[0] = load_rows("x0", x_rows[:, :, starts[0]:starts[0] + WIDTHS[0]])
-        w1_raw = load_rows("w1", k_rows(w1))
-        w3_raw = load_rows("w3", k_rows(w3))
-        x_raw[1] = load_rows("x1", x_rows[:, :, starts[1]:starts[1] + WIDTHS[1]])
-        x_raw[2] = load_rows("x2", x_rows[:, :, starts[2]:starts[2] + WIDTHS[2]])
-        wo_raw = load_rows("wo", k_rows(wo2))
+        raw = {}
+        sources = {"x0": x_rows[:, :, 0:256], "w1": k_rows(w1), "w2": k_rows(w2), "w3": k_rows(w3),
+                   "x12": x_rows[:, :, 256:512], "wo": k_rows(wo2)}
+        for i, name in enumerate(["x0","w2","w1","w3","x12","wo"]):
+            raw[name] = load_rows(name, sources[name])
+            if i == 0:
+                nc.sync.dma_start(out=hs_rows[0:P:ROWS, :, :], in_=hs.rearrange("g (b r) o -> b g (r o)", r=ROWS))
+        res_t = sb.tile([P, G, N], F32, name="res_t")
+        nc.sync.dma_start(out=res_t[:], in_=res.rearrange("g o n -> o g n"))
 
-        res_t, rows_t = {}, {}
-
-        def load_res(c):
-            res_t[c] = sb.tile([P, G, WIDTHS[c]], F32, name="res%d" % c)
-            nc.sync.dma_start(out=res_t[c][:],
-                              in_=res.rearrange("g o n -> o g n")[:, :, starts[c]:starts[c] + WIDTHS[c]])
-
-        load_res(0)
-
-        def prepare(name, raw):
-            packed = packed_tile(name, raw.shape[2])
-            interleave(nc.vector.tensor_copy, packed, raw, 0, raw.shape[2])
-            return quantize(name, packed)
-
-        nc.vector.transpose(out=hs_cols[:], in_=hs_rows[:].rearrange("p g r -> p (g r)"))
-        xq = {}
-        w2q = prepare("w2", w2_raw)
-        xq[0] = prepare("x0", x_raw[0])
+        xq, wq, hq, pk = {}, {}, {}, {}
         z2s, tt, uu, th, sg = {}, {}, {}, {}, {}
+        hh_rows = [sb.tile([P, PACK, w], BF16, name="hh_rows%d" % c) for c, w in enumerate(WIDTHS)]
+        y = [sb.tile([P, G, w], F32, name="y%d" % c) for c, w in enumerate(WIDTHS)]
 
         def work(name, s, dtype=F32):
             return sb.tile([P, WIDTHS[steps[s][0]]], dtype, name="%s%d" % (name, s))
 
-        def mm_z2(s):
-            c, g = steps[s]
-            product(bank_a[g], 0, w2q, xq[c], g, WIDTHS[c])
+        def mm_z(c, i, groups):
+            product(lambda g: z_at(c, i, g), wq[i], xq[c], groups)
 
-        def mm_z1(s):
-            c, g = steps[s]
-            product(bank_b[g], 0, w1q, xq[c], g, WIDTHS[c])
-
-        def mm_z3(s):
-            c, g = steps[s]
-            product(bank_a[g], HALF, w3q, xq[c], g, WIDTHS[c])
+        def mm_all(c, groups):
+            for i in (1, 2, 0):
+                mm_z(c, i, groups)
 
         def copy_z2(s):
-            c, g = steps[s]
             z2s[s] = work("z2s", s)
-            nc.scalar.copy(out=z2s[s][:], in_=bank_a[g][:, 0:WIDTHS[c]])
+            nc.scalar.copy(out=z2s[s][:], in_=z_at(steps[s][0], 1, steps[s][1]))
 
         def tanh_z3(s):
-            c, g = steps[s]
             th[s] = work("th", s)
-            nc.scalar.activation(out=th[s][:], in_=bank_a[g][:, HALF:HALF + WIDTHS[c]], func=ACT.Tanh)
+            nc.scalar.activation(out=th[s][:], in_=z_at(steps[s][0], 2, steps[s][1]), func=ACT.Tanh)
 
         def mul_z1(s):
-            c, g = steps[s]
             tt[s] = work("tt", s)
-            nc.vector.tensor_tensor(out=tt[s][:], in0=bank_b[g][:, 0:WIDTHS[c]], in1=z2s[s][:], op=ALU.mult)
+            nc.vector.tensor_tensor(out=tt[s][:], in0=z_at(steps[s][0], 0, steps[s][1]), in1=z2s[s][:], op=ALU.mult)
 
         def add_z3(s):
-            c, g = steps[s]
             uu[s] = work("uu", s)
-            nc.vector.tensor_tensor(out=uu[s][:], in0=bank_a[g][:, HALF:HALF + WIDTHS[c]], in1=tt[s][:], op=ALU.add)
+            nc.vector.tensor_tensor(out=uu[s][:], in0=z_at(steps[s][0], 2, steps[s][1]), in1=tt[s][:], op=ALU.add)
 
         def sigmoid(s):
             sg[s] = work("sg", s)
@@ -149,111 +142,110 @@ def tile_rows_fbilinsig_kernel(tc, x, w1, w2, w3, hs, wo2, res, out):
             hh = work("hh", s, BF16)
             nc.vector.scalar_tensor_tensor(out=hh[:], in0=sg[s][:], scalar=hs_cols[:, ROWS * g:ROWS * g + 1],
                                            in1=th[s][:], op0=ALU.mult, op1=ALU.mult)
-            if g == 0:
-                rows_t[c] = sb.tile([P, PACK, WIDTHS[c]], BF16, name="hh_rows%d" % c)
-            nc.sync.dma_start(out=rows_t[c][ROWS * g:ROWS * (g + 1), :, :], in_=hh[:])
-            if g == G - 1 and c + 1 < len(WIDTHS):
-                load_res(c + 1)
+            nc.sync.dma_start(out=hh_rows[c][ROWS * g:ROWS * (g + 1), :, :], in_=hh[:])
 
-        def y_bank(c, g):
-            return bank_a[g] if c % 2 else bank_b[g]
-
-        def mm_y(c, hq):
-            for g in range(G):
-                product(y_bank(c, g), HALF, woq, hq, g, WIDTHS[c])
-
-        y = {}
+        def mm_y(c):
+            product(lambda g: y_at(c, g), wq["o"], hq[c], range(G))
 
         def add_res(c, g):
-            if g == 0:
-                y[c] = sb.tile([P, G, WIDTHS[c]], F32, name="y%d" % c)
-            nc.vector.tensor_tensor(out=y[c][:, g, :], in0=y_bank(c, g)[:, HALF:HALF + WIDTHS[c]],
-                                    in1=res_t[c][:, g, :], op=ALU.add)
+            nc.vector.tensor_tensor(out=y[c][:, g, :], in0=y_at(c, g),
+                                    in1=res_t[:, g, STARTS[c]:STARTS[c] + WIDTHS[c]], op=ALU.add)
 
         def store(c, g0, g1):
-            nc.sync.dma_start(out=out.rearrange("g o n -> o g n")[:, g0:g1, starts[c]:starts[c] + WIDTHS[c]],
+            nc.sync.dma_start(out=out.rearrange("g o n -> o g n")[:, g0:g1, STARTS[c]:STARTS[c] + WIDTHS[c]],
                               in_=y[c][:, g0:g1, :])
 
-        for s in range(G):
-            mm_z2(s)
-        w1q = prepare("w1", w1_raw)
+        pk["x0"] = pack("x0", raw["x0"], 5)
+        nc.vector.transpose(out=hs_cols[:], in_=hs_rows[:].rearrange("p g r -> p (g r)"))
+        pk["w2"] = pack("w2", raw["w2"], 5)
+        xq[0] = quantize("x0", pk["x0"])
+        wq[1] = quantize("w2", pk["w2"])
+        mm_z(0, 1, range(G))
+        wq[0] = quantize("w1", pack("w1", raw["w1"], 5))
+        mm_z(0, 0, range(G))
         for s in range(G):
             copy_z2(s)
+        wq[2] = quantize("w3", pack("w3", raw["w3"], 8))
+        mm_z(0, 2, (0, 1))
+        mm_z(0, 2, (2, 3))
         for s in range(G):
-            mm_z1(s)
-        w3q = prepare("w3", w3_raw)
+            tanh_z3(s)
         for s in range(G):
-            mm_z3(s)
-        tanh_z3(0)
-
-        packed = {}
-        last = len(steps) - 1
-        for s in range(last + 3):
-            if s <= last:
-                mul_z1(s)
-            if s + 1 <= last:
-                if s + 1 >= G:
-                    copy_z2(s + 1)
-                tanh_z3(s + 1)
-            if 0 <= s - 2:
-                gate(s - 2)
-            if s <= last:
-                add_z3(s)
-            if 0 <= s - 1 <= last:
-                sigmoid(s - 1)
-            if s == 0:
-                packed["x1"] = packed_tile("x1", WIDTHS[1])
-                interleave(nc.vector.tensor_copy, packed["x1"], x_raw[1], 0, X1_VECTOR)
-                interleave(nc.scalar.copy, packed["x1"], x_raw[1], X1_VECTOR, WIDTHS[1])
+            mul_z1(s)
             if s == 1:
-                xq[1] = quantize("x1", packed["x1"])
-                mm_z2(G)
-                mm_z3(G)
-                mm_z1(G)
+                pk["x1"] = pack("x1", raw["x12"][:, :, 0:128], 8)
+        xq[1] = quantize("x1", pk["x1"])
+        mm_all(1, range(G))
+        pk["wo"] = pack("wo", raw["wo"], 0)
+        for s in range(G):
+            add_z3(s)
+            if s == 1:
+                pk["x2"] = pack("x2", raw["x12"][:, :, 128:256], 8)
+            sigmoid(s)
+            if s >= 1:
+                copy_z2(G + s - 1)
+                tanh_z3(G + s - 1)
+        xq[2] = quantize("x2", pk["x2"])
+        mm_all(2, range(G))
+        for s in range(G - 1, G):
+            copy_z2(G + s)
+            tanh_z3(G + s)
+        for s in range(2):
+            gate(s)
+        for s in range(G):
+            mul_z1(G + s)
+            if s + 2 < G:
+                gate(s + 2)
+            if s >= 1:
+                add_z3(G + s - 1)
             if s == 3:
-                packed["x2"] = packed_tile("x2", WIDTHS[2])
-                interleave(nc.scalar.copy, packed["x2"], x_raw[2], 0, WIDTHS[2])
-            if s == 4:
-                xq[2] = quantize("x2", packed["x2"])
-            if s == 5:
-                packed["wo"] = packed_tile("wo", O)
-                interleave(nc.scalar.copy, packed["wo"], wo_raw, 0, O)
-            if s == 6:
-                woq = quantize("wo", packed["wo"])
-            if s == 8:
-                packed["h0"] = packed_tile("h0", WIDTHS[0])
-                interleave(nc.scalar.copy, packed["h0"], rows_t[0], 0, WIDTHS[0])
-            if s == 10:
-                h0q = quantize("h0", packed["h0"])
-            if s >= 1 and s + G <= last:
-                mm_z2(s + G)
-                mm_z3(s + G)
-                mm_z1(s + G)
-        mm_y(0, h0q)
+                wq["o"] = quantize("wo", pk["wo"])
+        for s in range(G):
+            copy_z2(2 * G + s)
+            tanh_z3(2 * G + s)
+            if s == 0:
+                mul_z1(2 * G)
+                add_z3(2 * G - 1)
+            sigmoid(G + s)
 
-        packed["h1"] = packed_tile("h1", WIDTHS[1])
-        interleave(nc.vector.tensor_copy, packed["h1"], rows_t[1], 0, H1_VECTOR)
-        interleave(nc.scalar.copy, packed["h1"], rows_t[1], H1_VECTOR, WIDTHS[1])
-        add_res(0, 0)
-        add_res(0, 1)
-        h1q = quantize("h1", packed["h1"])
-        add_res(0, 2)
-        add_res(0, 3)
-        store(0, 0, G)
-        mm_y(1, h1q)
-        packed["h2"] = packed_tile("h2", WIDTHS[2])
-        interleave(nc.scalar.copy, packed["h2"], rows_t[2], 0, WIDTHS[2])
-        add_res(1, 0)
-        add_res(1, 1)
-        store(1, 0, 2)
-        h2q = quantize("h2", packed["h2"])
-        add_res(1, 2)
-        add_res(1, 3)
-        store(1, 2, G)
-        mm_y(2, h2q)
-        add_res(2, 0)
-        add_res(2, 1)
-        store(2, 0, 2)
-        add_res(2, 2)
-        add_res(2, 3)
-        store(2, 2, G)
+        for s in range(G):
+            if s >= 1:
+                mul_z1(2 * G + s)
+            gate(G + s)
+            if s >= 1:
+                add_z3(2 * G + s - 1)
+                sigmoid(2 * G + s - 1)
+            if s == 8:
+                pk["h0"] = pack("h0", hh_rows[0], 5)
+        add_z3(3 * G - 1)
+        sigmoid(3 * G - 1)
+        pk["h0"] = pack("h0", hh_rows[0], 5)
+        for s in range(G):
+            if s == 4:
+                hq[0] = quantize("h0", pk["h0"])
+                mm_y(0)
+            gate(2 * G + s)
+        hq[0] = quantize("h0", pk["h0"])
+        mm_y(0)
+        pk["h1"] = pack("h1", hh_rows[1], 0)
+        for g in range(G):
+            add_res(0, g)
+            if g == 1:
+                hq[1] = quantize("h1", pk["h1"])
+            if g % 2:
+                store(0, g - 1, g + 1)
+        mm_y(1)
+        for g in range(0):
+            add_res(1, g)
+            if g % 2:
+                store(1, g - 1, g + 1)
+        hq[2] = quantize("h2", pack("h2", hh_rows[2], 5))
+        mm_y(2)
+        for g in range(0, G):
+            add_res(1, g)
+            if g % 2:
+                store(1, g - 1, g + 1)
+        for g in range(G):
+            add_res(2, g)
+            if g % 2:
+                store(2, g - 1, g + 1)

from contextlib import ExitStack

import concourse.mybir as mybir

G, D, M, O, N = 4, 128, 128, 128, 512
FLOPS = 2 * G * N * (3 * D * M + M * O)

F32 = mybir.dt.float32
BF16 = mybir.dt.bfloat16
U32 = mybir.dt.uint32
U8 = mybir.dt.uint8
FP8X4 = mybir.dt.float8_e4m3fn_x4
ACT = mybir.ActivationFunctionType
ALU = mybir.AluOpType

P = 128
PACK = 4
ROWS = 32
NMM = 128
WIDTHS = (256, 128, 128)
STARTS = (0, 256, 384)


def tile_rows_fbilinsig_kernel(tc, x, w1, w2, w3, hs, wo2, res, out):
    nc = tc.nc
    steps = [(c, g) for c in range(len(WIDTHS)) for g in range(G)]

    with ExitStack() as ctx:
        sb = ctx.enter_context(tc.tile_pool(name="sb", bufs=1))
        ps = ctx.enter_context(tc.psum_pool(name="ps", bufs=1))
        ctx.enter_context(tc.manual_schedule())

        def load_rows(name, src):
            raw = sb.tile([P, PACK, src.shape[2]], F32, name=name + "_raw")
            nc.sync.dma_start(out=raw[:], in_=src)
            return raw

        def k_rows(t):
            return t.rearrange("g (p j) c -> (g p) j c", j=PACK)

        def interleave(copy, packed, raw, c0, c1):
            copy(out=packed[:, c0:c1, :].rearrange("p (c i) j -> p c j i", i=4),
                 in_=raw[:, :, c0:c1].rearrange("p j (c i) -> p c j i", i=4))

        def pack(name, raw, eighths):
            width = raw.shape[2]
            packed = sb.tile([P, width, PACK], BF16, name=name + "_packed", align_bytes=64)
            cut = width * eighths // 8
            if cut > 0:
                interleave(nc.vector.tensor_copy, packed, raw, 0, cut)
            if cut < width:
                interleave(nc.scalar.copy, packed, raw, cut, width)
            return packed

        def quantize(name, packed):
            width = packed.shape[1]
            codes = sb.tile([P, width], U32, name=name + "_codes", align_bytes=64)
            scales = sb.tile([P, width], U8, name=name + "_scales", align_bytes=64)
            nc.vector.quantize_mx(out=codes[:].bitcast(FP8X4), scales=scales[:],
                                  in_=packed[:].rearrange("p c j -> p (c j)"))
            return codes, scales

        def product(dsts, weights, moving, groups):
            width = moving[0].shape[1]
            for n0 in range(0, width, NMM):
                for g in groups:
                    rows = slice(ROWS * g, ROWS * (g + 1))
                    nc.tensor.matmul_mx(
                        out=dsts(g)[:, n0:n0 + NMM],
                        lhsT=weights[0][rows, :].bitcast(FP8X4), lhsT_scale=weights[1][rows, :],
                        rhs=moving[0][rows, n0:n0 + NMM].bitcast(FP8X4), rhs_scale=moving[1][rows, n0:n0 + NMM],
                        start=True, stop=True)

        banks = [[ps.tile([P, 512], F32, name="bank%d_%d" % (b, g)) for g in range(G)] for b in range(2)]
        z_place = {0: ((1, 0), (0, 0), (0, 256)), 1: ((1, 0), (1, 128), (1, 256)), 2: ((0, 0), (0, 128), (0, 256))}
        y_place = {0: (1, 0), 1: (0, 0), 2: (1, 256)}

        def z_at(c, i, g):
            b, col = z_place[c][i]
            return banks[b][g][:, col:col + WIDTHS[c]]

        def y_at(c, g):
            b, col = y_place[c]
            return banks[b][g][:, col:col + WIDTHS[c]]

        warm_in = sb.tile([P, 1], F32, name="warm_in")
        warm_out = sb.tile([P, 1], F32, name="warm_out")
        hs_rows = sb.tile([P, G, ROWS], F32, name="hs_rows", align_bytes=64)
        hs_cols = sb.tile([P, P], F32, name="hs_cols", align_bytes=64)
        nc.gpsimd.memset(hs_rows[:], 0.0)
        nc.vector.memset(warm_in[:], 0.0)
        nc.scalar.activation(out=warm_out[:], in_=warm_in[:], func=ACT.Sigmoid)

        x_rows = k_rows(x)
        raw = {}
        sources = {"x0": x_rows[:, :, 0:256], "w1": k_rows(w1), "w2": k_rows(w2), "w3": k_rows(w3),
                   "x12": x_rows[:, :, 256:512], "wo": k_rows(wo2)}
        for i, name in enumerate(["x0","w2","w1","w3","x12","wo"]):
            raw[name] = load_rows(name, sources[name])
            if i == 0:
                nc.sync.dma_start(out=hs_rows[0:P:ROWS, :, :], in_=hs.rearrange("g (b r) o -> b g (r o)", r=ROWS))
        res_t = sb.tile([P, G, N], F32, name="res_t")
        nc.sync.dma_start(out=res_t[:], in_=res.rearrange("g o n -> o g n"))

        xq, wq, hq, pk = {}, {}, {}, {}
        z2s, tt, uu, th, sg = {}, {}, {}, {}, {}
        hh_rows = [sb.tile([P, PACK, w], BF16, name="hh_rows%d" % c) for c, w in enumerate(WIDTHS)]
        y = [sb.tile([P, G, w], F32, name="y%d" % c) for c, w in enumerate(WIDTHS)]

        def work(name, s, dtype=F32):
            return sb.tile([P, WIDTHS[steps[s][0]]], dtype, name="%s%d" % (name, s))

        def mm_z(c, i, groups):
            product(lambda g: z_at(c, i, g), wq[i], xq[c], groups)

        def mm_all(c, groups):
            for i in (1, 2, 0):
                mm_z(c, i, groups)

        def copy_z2(s):
            z2s[s] = work("z2s", s)
            nc.scalar.copy(out=z2s[s][:], in_=z_at(steps[s][0], 1, steps[s][1]))

        def tanh_z3(s):
            th[s] = work("th", s)
            nc.scalar.activation(out=th[s][:], in_=z_at(steps[s][0], 2, steps[s][1]), func=ACT.Tanh)

        def mul_z1(s):
            tt[s] = work("tt", s)
            nc.vector.tensor_tensor(out=tt[s][:], in0=z_at(steps[s][0], 0, steps[s][1]), in1=z2s[s][:], op=ALU.mult)

        def add_z3(s):
            uu[s] = work("uu", s)
            nc.vector.tensor_tensor(out=uu[s][:], in0=z_at(steps[s][0], 2, steps[s][1]), in1=tt[s][:], op=ALU.add)

        def sigmoid(s):
            sg[s] = work("sg", s)
            nc.scalar.activation(out=sg[s][:], in_=uu[s][:], func=ACT.Sigmoid)

        def gate(s):
            c, g = steps[s]
            hh = work("hh", s, BF16)
            nc.vector.scalar_tensor_tensor(out=hh[:], in0=sg[s][:], scalar=hs_cols[:, ROWS * g:ROWS * g + 1],
                                           in1=th[s][:], op0=ALU.mult, op1=ALU.mult)
            nc.sync.dma_start(out=hh_rows[c][ROWS * g:ROWS * (g + 1), :, :], in_=hh[:])

        def mm_y(c):
            product(lambda g: y_at(c, g), wq["o"], hq[c], range(G))

        def add_res(c, g):
            nc.vector.tensor_tensor(out=y[c][:, g, :], in0=y_at(c, g),
                                    in1=res_t[:, g, STARTS[c]:STARTS[c] + WIDTHS[c]], op=ALU.add)

        def store(c, g0, g1):
            nc.sync.dma_start(out=out.rearrange("g o n -> o g n")[:, g0:g1, STARTS[c]:STARTS[c] + WIDTHS[c]],
                              in_=y[c][:, g0:g1, :])

        pk["x0"] = pack("x0", raw["x0"], 5)
        nc.vector.transpose(out=hs_cols[:], in_=hs_rows[:].rearrange("p g r -> p (g r)"))
        pk["w2"] = pack("w2", raw["w2"], 5)
        xq[0] = quantize("x0", pk["x0"])
        wq[1] = quantize("w2", pk["w2"])
        mm_z(0, 1, range(G))
        wq[0] = quantize("w1", pack("w1", raw["w1"], 5))
        mm_z(0, 0, range(G))
        for s in range(G):
            copy_z2(s)
        wq[2] = quantize("w3", pack("w3", raw["w3"], 8))
        mm_z(0, 2, (0, 1))
        mm_z(0, 2, (2, 3))
        for s in range(G):
            tanh_z3(s)
        for s in range(G):
            mul_z1(s)
            if s == 1:
                pk["x1"] = pack("x1", raw["x12"][:, :, 0:128], 8)
        xq[1] = quantize("x1", pk["x1"])
        mm_all(1, range(G))
        pk["wo"] = pack("wo", raw["wo"], 0)
        for s in range(G):
            add_z3(s)
            if s == 1:
                pk["x2"] = pack("x2", raw["x12"][:, :, 128:256], 8)
            sigmoid(s)
            if s >= 1:
                copy_z2(G + s - 1)
                tanh_z3(G + s - 1)
        xq[2] = quantize("x2", pk["x2"])
        mm_all(2, range(G))
        for s in range(G - 1, G):
            copy_z2(G + s)
            tanh_z3(G + s)
        for s in range(2):
            gate(s)
        for s in range(G):
            mul_z1(G + s)
            if s + 2 < G:
                gate(s + 2)
            if s >= 1:
                add_z3(G + s - 1)
            if s == 3:
                wq["o"] = quantize("wo", pk["wo"])
        for s in range(G):
            copy_z2(2 * G + s)
            tanh_z3(2 * G + s)
            if s == 0:
                mul_z1(2 * G)
                add_z3(2 * G - 1)
            sigmoid(G + s)

        for s in range(G):
            if s >= 1:
                mul_z1(2 * G + s)
            gate(G + s)
            if s >= 1:
                add_z3(2 * G + s - 1)
                sigmoid(2 * G + s - 1)
            if s == 8:
                pk["h0"] = pack("h0", hh_rows[0], 5)
        add_z3(3 * G - 1)
        sigmoid(3 * G - 1)
        pk["h0"] = pack("h0", hh_rows[0], 5)
        for s in range(G):
            if s == 4:
                hq[0] = quantize("h0", pk["h0"])
                mm_y(0)
            gate(2 * G + s)
        hq[0] = quantize("h0", pk["h0"])
        mm_y(0)
        pk["h1"] = pack("h1", hh_rows[1], 0)
        for g in range(G):
            add_res(0, g)
            if g == 1:
                hq[1] = quantize("h1", pk["h1"])
            if g % 2:
                store(0, g - 1, g + 1)
        mm_y(1)
        for g in range(0):
            add_res(1, g)
            if g % 2:
                store(1, g - 1, g + 1)
        hq[2] = quantize("h2", pack("h2", hh_rows[2], 5))
        mm_y(2)
        for g in range(0, G):
            add_res(1, g)
            if g % 2:
                store(1, g - 1, g + 1)
        for g in range(G):
            add_res(2, g)
            if g % 2:
                store(2, g - 1, g + 1)
